import numpy as np
import ml_dtypes


def mxq(x, axis, fmt="e4m3"):
    dtype, down = {"e4m3": (ml_dtypes.float8_e4m3fn, 7), "e5m2": (ml_dtypes.float8_e5m2, 14)}[fmt]
    v = np.moveaxis(np.asarray(x, np.float32).astype(ml_dtypes.bfloat16).astype(np.float64), axis, -1)
    blocks = v.reshape(v.shape[:-1] + (-1, 32))
    amax = np.abs(blocks).max(-1, keepdims=True)
    byte = np.maximum(np.where(amax > 0, np.frexp(amax)[1] - 1 + 127, 0) - down, 1)
    scale = np.exp2(byte - 127.0)
    codes = (blocks / scale).astype(np.float32).astype(dtype).astype(np.float64)
    return np.moveaxis((codes * scale).reshape(v.shape), -1, axis)


WIDE = False


def mx_kscale(k):
    if not WIDE:
        return np.ones(k)
    levels = np.array([10, -10, 5, -5, 0])
    if k % 512:
        return np.exp2(np.random.permutation(np.resize(levels, k // 32))).repeat(32)
    a = np.empty((k // 512, 16))
    for p in range(k // 512):
        a[p, :8] = np.random.permutation(np.resize(levels, 8))
        for g in range(8):
            far = levels[np.abs(levels - a[p, g]) >= 10]
            a[p, g + 8] = far[np.random.randint(len(far))]
    return np.exp2(a.ravel()).repeat(32)


def f64(x):
    return np.asarray(x).astype(np.float64)


def striped(idx):
    return np.tile(idx.reshape(-1, 16).T, (8, 1)).astype(np.uint16)


def unstriped(offs):
    return offs[:16].T.reshape(-1).astype(np.int64)


E2M1 = np.array([0.0, 0.5, 1.0, 1.5, 2.0, 3.0, 4.0, 6.0, -0.0, -0.5, -1.0, -1.5, -2.0, -3.0, -4.0, -6.0])


def pack_weight(w, fmt):
    k, n = w.shape
    w = f64(np.asarray(w, np.float32).astype(ml_dtypes.bfloat16)).reshape(k // 32, 32, n)
    amax = np.abs(w).max(1)
    if fmt == "e4m3":
        byte = np.frexp(amax)[1] - 1 + 127 - 7
    else:
        mant, ex = np.frexp(amax / 6.0)
        byte = np.where(mant > 0.5, ex, ex - 1) + 127
    byte = np.clip(np.where(amax > 0, byte, 1), 1, 254)
    scaled = (w * np.exp2(127.0 - byte)[:, None, :]).reshape(k, n).astype(np.float32)
    by_word = np.ascontiguousarray(scaled.reshape(k // 512, 128, 4, n).transpose(0, 1, 3, 2))
    if fmt == "e4m3":
        words = by_word.astype(ml_dtypes.float8_e4m3fn).view(np.uint8)
    else:
        c = by_word.astype(ml_dtypes.float4_e2m1fn).view(np.uint8) & 0xF
        words = (c[..., 0::2] | (c[..., 1::2] << 4)).reshape(k // 512, 128, 2 * n)
    return np.ascontiguousarray(words), np.ascontiguousarray(byte.astype(np.uint8).reshape(k // 512, 16, n))


def unpack_weight(words, scales, fmt):
    g, _, n = scales.shape
    words = np.ascontiguousarray(words).reshape(g, 128, n, -1)
    if fmt == "e4m3":
        vals = words.view(ml_dtypes.float8_e4m3fn).astype(np.float64)
    else:
        nib = np.empty((g, 128, n, 4), np.uint8)
        nib[..., 0::2] = words & 0xF
        nib[..., 1::2] = words >> 4
        vals = E2M1[nib]
    vals = vals * np.repeat(np.exp2(scales.astype(np.float64) - 127.0), 8, axis=1)[..., None]
    return vals.transpose(0, 1, 3, 2).reshape(g * 512, n)


def gelu(v):
    return 0.5 * v * (1.0 + np.tanh(np.sqrt(2.0 / np.pi) * (v + 0.044715 * v**3)))


K, T, S, H, T2, P, N = 1024, 4096, 1024, 512, 2048, 1024, 768

def setup_inputs():
    n = np.random.standard_normal
    s = mx_kscale(K)[:, None]
    u = mx_kscale(H)[:, None]
    d = {}
    d["tab_words"], d["tab_scales"] = pack_weight(n((K, T)) * s, "e4m3")
    d["offs"] = striped(np.random.permutation(T)[:S])
    d["w1"] = (n((K, H)) / s * 2.0 / K ** 0.5).astype(np.float32)
    d["w2_words"], d["w2_scales"] = pack_weight(n((K, H)) / s * 1.5 / K ** 0.5, "e2m1")
    d["gain"] = (np.exp(0.3 * n(H)) * u[:, 0]).astype(np.float32)
    d["wgs"] = np.exp(0.3 * n((128, S))).astype(np.float32)
    d["page0"] = (n((H, T2)) * u).astype(np.float32)
    d["offs2"] = striped(np.random.permutation(T2)[:S])
    d["offs3"] = striped(np.random.permutation(T2)[:P])
    d["w3"] = (n((K, H)) / s / u.T * 1.3 / K ** 0.5).astype(np.float32)
    d["gain2"] = (np.exp(0.3 * n(H)) * u[:, 0]).astype(np.float32)
    d["w4_words"], d["w4_scales"] = pack_weight(n((H, N)) / u * 1.6 / H ** 0.5, "e4m3")
    d["bias"] = (0.5 * n(N)).astype(np.float32)
    d["wgo"] = np.exp(0.3 * n((128, P))).astype(np.float32)
    d["page1"] = n((N, T2)).astype(np.float32)
    d["offs4"] = striped(np.random.permutation(T2)[:P])
    return d

def reference(tab_words, tab_scales, offs, w1, w2_words, w2_scales, gain, wgs, page0, offs2, offs3, w3, gain2, w4_words, w4_scales, bias, wgo, page1, offs4):
    v = unpack_weight(tab_words, tab_scales, "e4m3")[:, unstriped(offs)]
    a = mxq(f64(w1), 0, "e4m3").T @ v
    b = unpack_weight(w2_words, w2_scales, "e2m1").T @ v
    h = np.minimum(a / (1.0 + np.exp(-a)), b) * f64(gain)[:, None]
    page = f64(page0).copy()
    page[:, unstriped(offs2)] = np.tile(f64(wgs), (H // 128, 1)) * h
    skip = mxq(f64(w3), 0, "e4m3").T @ v
    x = page[:, unstriped(offs3)]
    z = np.tanh(x * skip) * f64(gain2)[:, None]
    y = (unpack_weight(w4_words, w4_scales, "e4m3").T @ mxq(z, 0, "e4m3")) + f64(bias)[:, None]
    out = f64(page1).copy()
    out[:, unstriped(offs4)] = np.tile(f64(wgo), (N // 128, 1)) * y
    return out

@@ -1,0 +1,270 @@
+from contextlib import ExitStack
+
+import concourse.mybir as mybir
+
+K, T, S, H, T2, N = 1024, 4096, 1024, 512, 2048, 768
+FLOPS = 2 * (3 * K * H * S + H * N * S)
+
+F32 = mybir.dt.float32
+BF16 = mybir.dt.bfloat16
+I32 = mybir.dt.int32
+U32 = mybir.dt.uint32
+U16 = mybir.dt.uint16
+U8 = mybir.dt.uint8
+FP8X4 = mybir.dt.float8_e4m3fn_x4
+FP4X4 = mybir.dt.float4_e2m1fn_x4
+ACT = mybir.ActivationFunctionType
+ALU = mybir.AluOpType
+
+P = 128
+PACK = 4
+PASSES = K // (P * PACK)
+QUADS = 4
+CHUNK = 512
+CHUNKS = S // CHUNK
+COLS = CHUNK // 16
+NT = N // P
+SCALE_BASE = 96
+
+
+def tile_list_stutter_session_page_kernel(
+    tc, tab_words, tab_scales, offs, w1, w2_words, w2_scales, gain, wgs, page0, offs2, offs3,
+    w3, gain2, w4_words, w4_scales, bias, wgo, page1, offs4, out,
+):
+    nc = tc.nc
+    with ExitStack() as ctx:
+        lists = ctx.enter_context(tc.tile_pool(name="lists", bufs=1))
+        keep = ctx.enter_context(tc.tile_pool(name="keep", bufs=1))
+        ring = ctx.enter_context(tc.tile_pool(name="ring", bufs=2))
+        psum = ctx.enter_context(tc.psum_pool(name="psum", bufs=2))
+
+        def held(shape, dtype, name):
+            return keep.tile(shape, dtype, name=name, align_bytes=64)
+
+        def load_list(src, name):
+            tile = lists.tile([P, S // 16], U16, name=name)
+            nc.sync.dma_start(tile[:], src)
+            return tile
+
+        def chunk_of(lst, c):
+            return lst[:, c * COLS : (c + 1) * COLS]
+
+        warm = held([P, 2], F32, "warm")
+        nc.vector.memset(warm[:, 0:1], 0.0)
+        nc.scalar.activation(warm[:, 1:2], warm[:, 0:1], ACT.Silu)
+        idx = load_list(offs, "idx")
+        tab_sc = held([P, T], U8, "tab_sc")
+        nc.vector.memset(tab_sc[0:SCALE_BASE, :].bitcast(I32), 0)
+        nc.sync.dma_start(
+            tab_sc[SCALE_BASE:P, :].bitcast(I32), tab_scales.rearrange("a q t -> (a q) t").bitcast(I32)
+        )
+        w2_sc_raw = held([P, PASSES, H], U8, "w2_sc_raw")
+        nc.gpsimd.memset(w2_sc_raw[:].rearrange("p a c -> p (a c)").bitcast(I32), 0)
+        v_sc = [held([P, S], U8, f"v_sc{a}") for a in range(PASSES)]
+        for a in range(PASSES):
+            nc.vector.memset(v_sc[a][:].bitcast(I32), 0)
+        w4_sc = held([P, N], U8, "w4_sc")
+        nc.vector.memset(w4_sc[:].bitcast(I32), 0)
+
+        picked_sc = held([P, S], U8, "picked_sc")
+        nc.vector.tensor_copy(picked_sc[:], tab_sc[:].indirect(idx[:]))
+
+        def place_scales(a):
+            for q in range(QUADS):
+                row = SCALE_BASE + 16 * a + 4 * q
+                nc.sync.dma_start(
+                    v_sc[a][32 * q : 32 * q + 4, :].bitcast(I32), picked_sc[row : row + 4, :].bitcast(I32)
+                )
+
+        def load_weight(w, a, tag):
+            raw = keep.tile([P, PACK, H], F32, name="raw", tag=tag, align_bytes=64)
+            nc.sync.dma_start(raw[:], w[a * 512 : (a + 1) * 512, :].rearrange("(p j) c -> p j c", j=PACK))
+            return raw
+
+        def quantize_weight(raw, rounded, name, copy):
+            copy(
+                rounded[:].rearrange("p (t m j) -> p m t j", t=PACK, j=PACK),
+                raw[:].rearrange("p j (m t) -> p m t j", t=PACK),
+            )
+            codes = held([P, H], U32, name + "_codes")
+            scales = held([P, H], U8, name + "_sc")
+            nc.vector.quantize_mx(codes[:].bitcast(FP8X4), scales[:], rounded[:])
+            return codes, scales
+
+        def load_w2_scales(quads):
+            for q in quads:
+                nc.sync.dma_start(
+                    w2_sc_raw[32 * q : 32 * q + 4].bitcast(I32),
+                    w2_scales[:, 4 * q : 4 * q + 4, :].rearrange("a r c -> r a c").bitcast(I32),
+                )
+
+        def load_table(a):
+            table = keep.tile([P, T], I32, name="table", tag=f"table{a}", align_bytes=64)
+            nc.sync.dma_start(table[:], tab_words[a].rearrange("p t i -> p (t i)").bitcast(I32))
+            return table
+
+        w1_raw = [load_weight(w1, a, f"session{2 + a}") for a in range(PASSES)]
+        w2_raw = held([P, PASSES, 2 * H], U8, "w2_raw")
+        nc.sync.dma_start(w2_raw[:].bitcast(I32), w2_words.rearrange("a p c -> p a c").bitcast(I32))
+        gain_sb = held([P, PACK], F32, "gain_sb")
+        nc.sync.dma_start(gain_sb[:], gain.rearrange("(p t) -> p t", t=PACK))
+        idx2 = load_list(offs2, "idx2")
+        idx3 = load_list(offs3, "idx3")
+        load_w2_scales((0, 1))
+        tables = [load_table(0)]
+        load_w2_scales((2, 3))
+        place_scales(0)
+        tables.append(load_table(1))
+        place_scales(1)
+
+        w1_q = []
+        for a, copy in enumerate((nc.vector.tensor_copy, nc.scalar.copy)):
+            rounded = ring.tile([P, PACK * H], BF16, name="rounded", tag="rounded", align_bytes=64)
+            w1_q.append(quantize_weight(w1_raw[a], rounded, f"w1{a}", copy))
+
+        w2_codes = held([P, PASSES, 2 * H], U8, "w2_codes")
+        for a in range(PASSES):
+            nc.vector.tensor_copy(
+                w2_codes[:, a, :].rearrange("p (t m b) -> p t m b", t=PACK, b=2),
+                w2_raw[:, a, :].rearrange("p (m t b) -> p t m b", t=PACK, b=2),
+            )
+        w2_sc = held([P, PASSES, H], U8, "w2_sc")
+        nc.vector.tensor_copy(
+            w2_sc[:].rearrange("p a (t m) -> p a t m", t=PACK),
+            w2_sc_raw[:].rearrange("p a (m t) -> p a t m", t=PACK),
+        )
+
+        v = {}
+        for a in range(PASSES):
+            for c in range(CHUNKS):
+                v[a, c] = held([P, CHUNK], U32, f"v{a}{c}")
+                nc.vector.tensor_copy(v[a, c][:], tables[a][:].bitcast(U32).indirect(chunk_of(idx, c)))
+
+        def first_stage(tag, c, weights):
+            bank = psum.tile([P, CHUNK], F32, name=tag, tag=tag)
+            for a in range(PASSES):
+                lhs, lhs_sc = weights(a)
+                nc.tensor.matmul_mx(
+                    bank[:], lhsT=lhs, lhsT_scale=lhs_sc,
+                    rhs=v[a, c][:].bitcast(FP8X4), rhs_scale=v_sc[a][:, c * CHUNK : (c + 1) * CHUNK],
+                    start=(a == 0), stop=(a == PASSES - 1),
+                )
+            return bank
+
+        def e4m3_slice(q, t):
+            return lambda a: (q[a][0][:, t * P : (t + 1) * P].bitcast(FP8X4), q[a][1][:, t * P : (t + 1) * P])
+
+        def w2_slice(t):
+            return lambda a: (
+                w2_codes[:, a, 2 * t * P : 2 * (t + 1) * P].bitcast(FP4X4), w2_sc[:, a, t * P : (t + 1) * P]
+            )
+
+        wgs_rows = wgs.rearrange("(q t) j -> q t j", t=PACK)
+        page0_rows = page0.rearrange("(p t) j -> p t j", t=PACK)
+        pages = [held([P, T2], F32, f"page{t}") for t in range(PACK)]
+        nc.sync.dma_start(pages[0][:], page0_rows[:, 0, :])
+        wg_first = keep.tile([P, S], F32, name="wg_first", tag="wg_first", align_bytes=64)
+        for q in range(QUADS):
+            nc.sync.dma_start(wg_first[32 * q : 32 * (q + 1), :], wgs_rows[:, 0, :])
+        wg_rest = keep.tile([P, PACK - 1, S], F32, name="wg_rest", tag="wg_rest", align_bytes=64)
+        for q in range(QUADS):
+            nc.sync.dma_start(wg_rest[32 * q : 32 * (q + 1), :, :], wgs_rows[:, 1:PACK, :])
+        wg = [wg_first[:]] + [wg_rest[:, t - 1, :] for t in range(1, PACK)]
+        nc.sync.dma_start(pages[1][:], page0_rows[:, 1, :])
+        w3_raw = [load_weight(w3, a, f"session{4 + a}") for a in range(PASSES)]
+        for t in range(2, PACK):
+            nc.sync.dma_start(pages[t][:], page0_rows[:, t, :])
+        gain2_sb = held([P, PACK], F32, "gain2_sb")
+        nc.sync.dma_start(gain2_sb[:], gain2.rearrange("(p t) -> p t", t=PACK))
+        idx4 = load_list(offs4, "idx4")
+        w4_codes = held([P, N], I32, "w4_codes")
+        nc.sync.dma_start(w4_codes[:], w4_words[0].rearrange("p c i -> p (c i)").bitcast(I32))
+        for q in range(QUADS):
+            nc.sync.dma_start(
+                w4_sc[32 * q : 32 * q + 4, :].bitcast(I32), w4_scales[0, 4 * q : 4 * q + 4, :].bitcast(I32)
+            )
+        wgo_sb = held([P, S], F32, "wgo_sb")
+        nc.sync.dma_start(wgo_sb[:], wgo)
+        bias_sb = held([P, NT], F32, "bias_sb")
+        with nc.allow_non_contiguous_dma(reason="one bias value for each partition and row tile"):
+            nc.sync.dma_start(bias_sb[:], bias.rearrange("(i p) -> p i", p=P))
+
+        scaled = keep.tile([P, PACK, S], F32, name="scaled", tag="table1", align_bytes=64)
+        for t in range(PACK):
+            least = keep.tile([P, S], F32, name="least", tag=f"least{t}", align_bytes=64)
+            for c in range(CHUNKS):
+                cols = slice(c * CHUNK, (c + 1) * CHUNK)
+                a_bank = first_stage("a_bank", c, e4m3_slice(w1_q, t))
+                b_bank = first_stage("b_bank", c, w2_slice(t))
+                nc.scalar.activation(least[:, cols], a_bank[:], ACT.Silu)
+                nc.scalar.activation(scaled[:, t, cols], wg[t][:, cols], ACT.Copy, scale=gain_sb[:, t : t + 1])
+                nc.vector.tensor_tensor(least[:, cols], b_bank[:], least[:, cols], ALU.min)
+                if t == 0:
+                    nc.vector.tensor_tensor(pages[t][:].indirect(chunk_of(idx2, c)), least[:, cols], scaled[:, t, cols], ALU.mult)
+            if t > 0:
+                nc.vector.tensor_tensor(pages[t][:].indirect(idx2[:]), least[:], scaled[:, t, :], ALU.mult)
+        w3_q = []
+        for a in range(PASSES):
+            rounded = keep.tile([P, PACK * H], BF16, name="rounded", tag=f"least{a}", align_bytes=64)
+            w3_q.append(quantize_weight(w3_raw[a], rounded, f"w3{a}", nc.scalar.copy))
+        session = [keep.tile([P, T2], F32, name="session", tag=f"session{i}", align_bytes=64) for i in range(NT)]
+        for i in range(NT):
+            nc.sync.dma_start(session[i][:], page1[i * P : (i + 1) * P, :])
+        skip = keep.tile([P, PACK, S], F32, name="skip", tag="table0", align_bytes=64)
+        for c in range(CHUNKS):
+            for t in range(PACK):
+                bank = first_stage("skip_bank", c, e4m3_slice(w3_q, t))
+                nc.scalar.copy(skip[:, t, c * CHUNK : (c + 1) * CHUNK], bank[:])
+
+        spans = [(0, 256), (256, 512), (512, 1024)]
+        first = spans[0][1]
+        prod_first = keep.tile([P, PACK, first], F32, name="prod_first", tag="wg_first", align_bytes=64)
+        prod_rest = keep.tile([P, PACK, S - first], F32, name="prod_rest", tag="table1", align_bytes=64)
+
+        def weave(n):
+            lo, hi = spans[n]
+            prod = prod_first[:] if n == 0 else prod_rest[:, :, lo - first : hi - first]
+            curved = prod
+            if n == 1:
+                curved = keep.tile([P, PACK, hi - lo], F32, name="curved", tag="planes0", align_bytes=64)[:]
+            planes = keep.tile([P, PACK, hi - lo], BF16, name="planes", tag=f"planes{n}", align_bytes=64)
+            for t in range(PACK):
+                nc.vector.tensor_tensor(
+                    prod[:, t, :], pages[t][:].indirect(idx3[:, lo // 16 : hi // 16]), skip[:, t, lo:hi], ALU.mult
+                )
+                nc.scalar.activation(curved[:, t, :], prod[:, t, :], ACT.Tanh)
+                nc.scalar.activation(planes[:, t, :], curved[:, t, :], ACT.Copy, scale=gain2_sb[:, t : t + 1])
+            woven = ring.tile([P, hi - lo, PACK], BF16, name="woven", tag="rounded", align_bytes=64)
+            nc.scalar.copy(
+                woven[:].rearrange("p (g i) t -> p g t i", i=4),
+                planes[:].rearrange("p t (g i) -> p g t i", i=4),
+            )
+            z_codes = held([P, hi - lo], U32, f"z_codes{n}")
+            z_sc = held([P, hi - lo], U8, f"z_sc{n}")
+            nc.vector.quantize_mx(z_codes[:].bitcast(FP8X4), z_sc[:], woven[:].rearrange("p j t -> p (j t)"))
+            return z_codes, z_sc
+
+        def put(n, i, z, y):
+            lo, hi = spans[n]
+            y_bank = psum.tile([P, hi - lo], F32, name="y_bank", tag="y_bank")
+            nc.tensor.matmul_mx(
+                y_bank[:], lhsT=w4_codes[:, i * P : (i + 1) * P].bitcast(FP8X4),
+                lhsT_scale=w4_sc[:, i * P : (i + 1) * P],
+                rhs=z[0][:].bitcast(FP8X4), rhs_scale=z[1][:], start=True, stop=True,
+            )
+            nc.scalar.activation(y[:], y_bank[:], ACT.Identity, bias=bias_sb[:, i : i + 1])
+            nc.vector.tensor_tensor(
+                session[i][:].indirect(idx4[:, lo // 16 : hi // 16]), y[:], wgo_sb[:, lo:hi], ALU.mult
+            )
+            if hi == S:
+                nc.sync.dma_start(out[i * P : (i + 1) * P, :], session[i][:])
+
+        z = weave(0)
+        for n, (lo, hi) in enumerate(spans):
+            last = n == len(spans) - 1
+            for i in range(NT if last else NT - 1):
+                put(n, i, z, ring.tile([P, hi - lo], F32, name="y", tag="y", bufs=NT))
+            if not last:
+                z_next = weave(n + 1)
+                put(n, NT - 1, z, keep.tile([P, hi - lo], F32, name="y_held", tag=f"planes{n + 1}", align_bytes=64))
+                z = z_next

@@ -62,9 +62,9 @@ def tile_list_stutter_session_page_kernel(
         nc.gpsimd.memset(w2_sc_raw[:].rearrange("p a c -> p (a c)").bitcast(I32), 0)
         v_sc = [held([P, S], U8, f"v_sc{a}") for a in range(PASSES)]
         for a in range(PASSES):
-            nc.vector.memset(v_sc[a][:].bitcast(I32), 0)
+            nc.gpsimd.memset(v_sc[a][:].bitcast(I32), 0)
         w4_sc = held([P, N], U8, "w4_sc")
-        nc.vector.memset(w4_sc[:].bitcast(I32), 0)
+        nc.gpsimd.memset(w4_sc[:].bitcast(I32), 0)
 
         picked_sc = held([P, S], U8, "picked_sc")
         nc.vector.tensor_copy(picked_sc[:], tab_sc[:].indirect(idx[:]))
@@ -81,8 +81,8 @@ def tile_list_stutter_session_page_kernel(
             nc.sync.dma_start(raw[:], w[a * 512 : (a + 1) * 512, :].rearrange("(p j) c -> p j c", j=PACK))
             return raw
 
-        def quantize_weight(raw, rounded, name, copy):
-            copy(
+        def quantize_weight(raw, rounded, name):
+            nc.scalar.copy(
                 rounded[:].rearrange("p (t m j) -> p m t j", t=PACK, j=PACK),
                 raw[:].rearrange("p j (m t) -> p m t j", t=PACK),
             )
@@ -110,17 +110,17 @@ def tile_list_stutter_session_page_kernel(
         nc.sync.dma_start(gain_sb[:], gain.rearrange("(p t) -> p t", t=PACK))
         idx2 = load_list(offs2, "idx2")
         idx3 = load_list(offs3, "idx3")
-        load_w2_scales((0, 1))
+        load_w2_scales((0, 2))
         tables = [load_table(0)]
-        load_w2_scales((2, 3))
+        load_w2_scales((1, 3))
         place_scales(0)
         tables.append(load_table(1))
         place_scales(1)
 
         w1_q = []
-        for a, copy in enumerate((nc.vector.tensor_copy, nc.scalar.copy)):
+        for a in range(PASSES):
             rounded = ring.tile([P, PACK * H], BF16, name="rounded", tag="rounded", align_bytes=64)
-            w1_q.append(quantize_weight(w1_raw[a], rounded, f"w1{a}", copy))
+            w1_q.append(quantize_weight(w1_raw[a], rounded, f"w1{a}"))
 
         w2_codes = held([P, PASSES, 2 * H], U8, "w2_codes")
         for a in range(PASSES):
@@ -164,14 +164,15 @@ def tile_list_stutter_session_page_kernel(
         pages = [held([P, T2], F32, f"page{t}") for t in range(PACK)]
         nc.sync.dma_start(pages[0][:], page0_rows[:, 0, :])
         wg_first = keep.tile([P, S], F32, name="wg_first", tag="wg_first", align_bytes=64)
-        for q in range(QUADS):
+        for q in (0, 2, 1, 3):
             nc.sync.dma_start(wg_first[32 * q : 32 * (q + 1), :], wgs_rows[:, 0, :])
+        w3_raw = [load_weight(w3, 0, "session4")]
         wg_rest = keep.tile([P, PACK - 1, S], F32, name="wg_rest", tag="wg_rest", align_bytes=64)
-        for q in range(QUADS):
+        for q in (0, 2, 1, 3):
             nc.sync.dma_start(wg_rest[32 * q : 32 * (q + 1), :, :], wgs_rows[:, 1:PACK, :])
         wg = [wg_first[:]] + [wg_rest[:, t - 1, :] for t in range(1, PACK)]
         nc.sync.dma_start(pages[1][:], page0_rows[:, 1, :])
-        w3_raw = [load_weight(w3, a, f"session{4 + a}") for a in range(PASSES)]
+        w3_raw.append(load_weight(w3, 1, "session5"))
         for t in range(2, PACK):
             nc.sync.dma_start(pages[t][:], page0_rows[:, t, :])
         gain2_sb = held([P, PACK], F32, "gain2_sb")
@@ -190,23 +191,36 @@ def tile_list_stutter_session_page_kernel(
             nc.sync.dma_start(bias_sb[:], bias.rearrange("(i p) -> p i", p=P))
 
         scaled = keep.tile([P, PACK, S], F32, name="scaled", tag="table1", align_bytes=64)
-        for t in range(PACK):
-            least = keep.tile([P, S], F32, name="least", tag=f"least{t}", align_bytes=64)
+
+        def new_states(t, c, least):
+            cols = slice(c * CHUNK, (c + 1) * CHUNK)
+            a_bank = first_stage("a_bank", c, e4m3_slice(w1_q, t))
+            b_bank = first_stage("b_bank", c, w2_slice(t))
+            nc.scalar.activation(least, a_bank[:], ACT.Silu)
+            nc.scalar.activation(scaled[:, t, cols], wg[t][:, cols], ACT.Copy, scale=gain_sb[:, t : t + 1])
+            nc.vector.tensor_tensor(least, b_bank[:], least, ALU.min)
+
+        def renew(t):
+            least = held([P, S], F32, f"least{t}")
             for c in range(CHUNKS):
-                cols = slice(c * CHUNK, (c + 1) * CHUNK)
-                a_bank = first_stage("a_bank", c, e4m3_slice(w1_q, t))
-                b_bank = first_stage("b_bank", c, w2_slice(t))
-                nc.scalar.activation(least[:, cols], a_bank[:], ACT.Silu)
-                nc.scalar.activation(scaled[:, t, cols], wg[t][:, cols], ACT.Copy, scale=gain_sb[:, t : t + 1])
-                nc.vector.tensor_tensor(least[:, cols], b_bank[:], least[:, cols], ALU.min)
-                if t == 0:
-                    nc.vector.tensor_tensor(pages[t][:].indirect(chunk_of(idx2, c)), least[:, cols], scaled[:, t, cols], ALU.mult)
-            if t > 0:
-                nc.vector.tensor_tensor(pages[t][:].indirect(idx2[:]), least[:], scaled[:, t, :], ALU.mult)
-        w3_q = []
-        for a in range(PASSES):
-            rounded = keep.tile([P, PACK * H], BF16, name="rounded", tag=f"least{a}", align_bytes=64)
-            w3_q.append(quantize_weight(w3_raw[a], rounded, f"w3{a}", nc.scalar.copy))
+                new_states(t, c, least[:, c * CHUNK : (c + 1) * CHUNK])
+            nc.vector.tensor_tensor(pages[t][:].indirect(idx2[:]), least[:], scaled[:, t, :], ALU.mult)
+
+        def quantize_w3(a):
+            rounded = keep.tile([P, PACK * H], BF16, name="rounded", tag=f"first{a}", align_bytes=64)
+            return quantize_weight(w3_raw[a], rounded, f"w3{a}")
+
+        for c in range(CHUNKS):
+            least = keep.tile([P, CHUNK], F32, name="least", tag=f"first{c}", align_bytes=64)
+            new_states(0, c, least[:])
+            nc.vector.tensor_tensor(
+                pages[0][:].indirect(chunk_of(idx2, c)), least[:], scaled[:, 0, c * CHUNK : (c + 1) * CHUNK], ALU.mult
+            )
+        w3_q = [quantize_w3(0)]
+        renew(1)
+        w3_q.append(quantize_w3(1))
+        renew(2)
+        renew(3)
         session = [keep.tile([P, T2], F32, name="session", tag=f"session{i}", align_bytes=64) for i in range(NT)]
         for i in range(NT):
             nc.sync.dma_start(session[i][:], page1[i * P : (i + 1) * P, :])
@@ -217,13 +231,11 @@ def tile_list_stutter_session_page_kernel(
                 nc.scalar.copy(skip[:, t, c * CHUNK : (c + 1) * CHUNK], bank[:])
 
         spans = [(0, 256), (256, 512), (512, 1024)]
-        first = spans[0][1]
-        prod_first = keep.tile([P, PACK, first], F32, name="prod_first", tag="wg_first", align_bytes=64)
-        prod_rest = keep.tile([P, PACK, S - first], F32, name="prod_rest", tag="table1", align_bytes=64)
+        prods = keep.tile([P, PACK, S], F32, name="prods", tag="table1", align_bytes=64)
 
         def weave(n):
             lo, hi = spans[n]
-            prod = prod_first[:] if n == 0 else prod_rest[:, :, lo - first : hi - first]
+            prod = prods[:, :, lo:hi]
             curved = prod
             if n == 1:
                 curved = keep.tile([P, PACK, hi - lo], F32, name="curved", tag="planes0", align_bytes=64)[:]

@@ -25,6 +25,7 @@ CHUNKS = S // CHUNK
 COLS = CHUNK // 16
 NT = N // P
 SCALE_BASE = 96
+BANKS = {"a_bank": 2, "b_bank": 6}
 
 
 def tile_list_stutter_session_page_kernel(
@@ -69,8 +70,8 @@ def tile_list_stutter_session_page_kernel(
         picked_sc = held([P, S], U8, "picked_sc")
         nc.vector.tensor_copy(picked_sc[:], tab_sc[:].indirect(idx[:]))
 
-        def place_scales(a):
-            for q in range(QUADS):
+        def place_scales(a, quads):
+            for q in quads:
                 row = SCALE_BASE + 16 * a + 4 * q
                 nc.sync.dma_start(
                     v_sc[a][32 * q : 32 * q + 4, :].bitcast(I32), picked_sc[row : row + 4, :].bitcast(I32)
@@ -81,14 +82,13 @@ def tile_list_stutter_session_page_kernel(
             nc.sync.dma_start(raw[:], w[a * 512 : (a + 1) * 512, :].rearrange("(p j) c -> p j c", j=PACK))
             return raw
 
-        def quantize_weight(raw, rounded, name):
+        def quantize_weight(raw, rounded, codes, name):
             nc.scalar.copy(
-                rounded[:].rearrange("p (t m j) -> p m t j", t=PACK, j=PACK),
+                rounded.rearrange("p (t m j) -> p m t j", t=PACK, j=PACK),
                 raw[:].rearrange("p j (m t) -> p m t j", t=PACK),
             )
-            codes = held([P, H], U32, name + "_codes")
             scales = held([P, H], U8, name + "_sc")
-            nc.vector.quantize_mx(codes[:].bitcast(FP8X4), scales[:], rounded[:])
+            nc.vector.quantize_mx(codes.bitcast(FP8X4), scales[:], rounded)
             return codes, scales
 
         def load_w2_scales(quads):
@@ -107,20 +107,20 @@ def tile_list_stutter_session_page_kernel(
         w2_raw = held([P, PASSES, 2 * H], U8, "w2_raw")
         nc.sync.dma_start(w2_raw[:].bitcast(I32), w2_words.rearrange("a p c -> p a c").bitcast(I32))
         gain_sb = held([P, PACK], F32, "gain_sb")
-        nc.sync.dma_start(gain_sb[:], gain.rearrange("(p t) -> p t", t=PACK))
+        nc.gpsimd.dma_start(gain_sb[:], gain.rearrange("(p t) -> p t", t=PACK))
         idx2 = load_list(offs2, "idx2")
-        idx3 = load_list(offs3, "idx3")
-        load_w2_scales((0, 2))
+        load_w2_scales((0, 2, 1, 3))
         tables = [load_table(0)]
-        load_w2_scales((1, 3))
-        place_scales(0)
+        place_scales(0, (0, 2, 1, 3))
+        place_scales(1, (0, 2))
         tables.append(load_table(1))
-        place_scales(1)
+        place_scales(1, (1, 3))
 
         w1_q = []
         for a in range(PASSES):
             rounded = ring.tile([P, PACK * H], BF16, name="rounded", tag="rounded", align_bytes=64)
-            w1_q.append(quantize_weight(w1_raw[a], rounded, f"w1{a}"))
+            codes = held([P, H], U32, f"w1_codes{a}")
+            w1_q.append(quantize_weight(w1_raw[a], rounded[:], codes[:], f"w1{a}"))
 
         w2_codes = held([P, PASSES, 2 * H], U8, "w2_codes")
         for a in range(PASSES):
@@ -141,7 +141,7 @@ def tile_list_stutter_session_page_kernel(
                 nc.vector.tensor_copy(v[a, c][:], tables[a][:].bitcast(U32).indirect(chunk_of(idx, c)))
 
         def first_stage(tag, c, weights):
-            bank = psum.tile([P, CHUNK], F32, name=tag, tag=tag)
+            bank = psum.tile([P, CHUNK], F32, name="bank", tag=tag, bufs=BANKS[tag])
             for a in range(PASSES):
                 lhs, lhs_sc = weights(a)
                 nc.tensor.matmul_mx(
@@ -159,24 +159,28 @@ def tile_list_stutter_session_page_kernel(
                 w2_codes[:, a, 2 * t * P : 2 * (t + 1) * P].bitcast(FP4X4), w2_sc[:, a, t * P : (t + 1) * P]
             )
 
-        wgs_rows = wgs.rearrange("(q t) j -> q t j", t=PACK)
+        wgs_rows = wgs.rearrange("(q t) j -> q (t j)", t=PACK)
         page0_rows = page0.rearrange("(p t) j -> p t j", t=PACK)
         pages = [held([P, T2], F32, f"page{t}") for t in range(PACK)]
+        wg = {}
+
+        def load_wgs(first, last):
+            tile = held([P, (last - first) * CHUNK], F32, f"wgs{first}")
+            for q in (0, 2, 1, 3):
+                nc.sync.dma_start(tile[32 * q : 32 * (q + 1), :], wgs_rows[:, first * CHUNK : last * CHUNK])
+            for n in range(first, last):
+                wg[divmod(n, CHUNKS)] = tile[:, (n - first) * CHUNK : (n - first + 1) * CHUNK]
+
+        load_wgs(0, 1)
         nc.sync.dma_start(pages[0][:], page0_rows[:, 0, :])
-        wg_first = keep.tile([P, S], F32, name="wg_first", tag="wg_first", align_bytes=64)
-        for q in (0, 2, 1, 3):
-            nc.sync.dma_start(wg_first[32 * q : 32 * (q + 1), :], wgs_rows[:, 0, :])
-        w3_raw = [load_weight(w3, 0, "session4")]
-        wg_rest = keep.tile([P, PACK - 1, S], F32, name="wg_rest", tag="wg_rest", align_bytes=64)
-        for q in (0, 2, 1, 3):
-            nc.sync.dma_start(wg_rest[32 * q : 32 * (q + 1), :, :], wgs_rows[:, 1:PACK, :])
-        wg = [wg_first[:]] + [wg_rest[:, t - 1, :] for t in range(1, PACK)]
-        nc.sync.dma_start(pages[1][:], page0_rows[:, 1, :])
-        w3_raw.append(load_weight(w3, 1, "session5"))
-        for t in range(2, PACK):
+        load_wgs(1, 4)
+        load_wgs(4, 8)
+        w3_raw = [load_weight(w3, a, f"session{4 + a}") for a in range(PASSES)]
+        for t in range(1, PACK):
             nc.sync.dma_start(pages[t][:], page0_rows[:, t, :])
         gain2_sb = held([P, PACK], F32, "gain2_sb")
         nc.sync.dma_start(gain2_sb[:], gain2.rearrange("(p t) -> p t", t=PACK))
+        idx3 = load_list(offs3, "idx3")
         idx4 = load_list(offs4, "idx4")
         w4_codes = held([P, N], I32, "w4_codes")
         nc.sync.dma_start(w4_codes[:], w4_words[0].rearrange("p c i -> p (c i)").bitcast(I32))
@@ -190,62 +194,67 @@ def tile_list_stutter_session_page_kernel(
         with nc.allow_non_contiguous_dma(reason="one bias value for each partition and row tile"):
             nc.sync.dma_start(bias_sb[:], bias.rearrange("(i p) -> p i", p=P))
 
-        scaled = keep.tile([P, PACK, S], F32, name="scaled", tag="table1", align_bytes=64)
-
-        def new_states(t, c, least):
-            cols = slice(c * CHUNK, (c + 1) * CHUNK)
+        def new_states(t, c, least, scaled):
             a_bank = first_stage("a_bank", c, e4m3_slice(w1_q, t))
             b_bank = first_stage("b_bank", c, w2_slice(t))
             nc.scalar.activation(least, a_bank[:], ACT.Silu)
-            nc.scalar.activation(scaled[:, t, cols], wg[t][:, cols], ACT.Copy, scale=gain_sb[:, t : t + 1])
+            nc.scalar.activation(scaled, wg[t, c], ACT.Copy, scale=gain_sb[:, t : t + 1])
             nc.vector.tensor_tensor(least, b_bank[:], least, ALU.min)
 
-        def renew(t):
-            least = held([P, S], F32, f"least{t}")
+        def renew(t, least_tag):
+            least = keep.tile([P, S], F32, name="least", tag=least_tag, align_bytes=64)
             for c in range(CHUNKS):
-                new_states(t, c, least[:, c * CHUNK : (c + 1) * CHUNK])
-            nc.vector.tensor_tensor(pages[t][:].indirect(idx2[:]), least[:], scaled[:, t, :], ALU.mult)
-
-        def quantize_w3(a):
-            rounded = keep.tile([P, PACK * H], BF16, name="rounded", tag=f"first{a}", align_bytes=64)
-            return quantize_weight(w3_raw[a], rounded, f"w3{a}")
+                cols = slice(c * CHUNK, (c + 1) * CHUNK)
+                new_states(t, c, least[:, cols], scaled_rest[:, t - 1, cols])
+            nc.vector.tensor_tensor(pages[t][:].indirect(idx2[:]), least[:], scaled_rest[:, t - 1, :], ALU.mult)
 
         for c in range(CHUNKS):
-            least = keep.tile([P, CHUNK], F32, name="least", tag=f"first{c}", align_bytes=64)
-            new_states(0, c, least[:])
-            nc.vector.tensor_tensor(
-                pages[0][:].indirect(chunk_of(idx2, c)), least[:], scaled[:, 0, c * CHUNK : (c + 1) * CHUNK], ALU.mult
+            least = keep.tile([P, CHUNK], F32, name="least", tag=f"least0{c}", align_bytes=64)
+            scaled = keep.tile([P, CHUNK], F32, name="scaled", tag=f"scaled0{c}", align_bytes=64)
+            new_states(0, c, least[:], scaled[:])
+            nc.vector.tensor_tensor(pages[0][:].indirect(chunk_of(idx2, c)), least[:], scaled[:], ALU.mult)
+        scaled_rest = keep.tile([P, PACK - 1, S], F32, name="scaled_rest", tag="least00", align_bytes=64)
+        renew(1, "least1")
+        renew(2, "least2")
+        renew(3, "table1")
+        w3_rounded = keep.tile([P, PASSES * PACK * H], BF16, name="w3_rounded", tag="scaled00", align_bytes=64)
+        w3_codes = keep.tile([P, PASSES * H], U32, name="w3_codes", tag="least1", align_bytes=64)
+        w3_q = [
+            quantize_weight(
+                w3_raw[a], w3_rounded[:, a * PACK * H : (a + 1) * PACK * H], w3_codes[:, a * H : (a + 1) * H], f"w3{a}"
             )
-        w3_q = [quantize_w3(0)]
-        renew(1)
-        w3_q.append(quantize_w3(1))
-        renew(2)
-        renew(3)
+            for a in range(PASSES)
+        ]
         session = [keep.tile([P, T2], F32, name="session", tag=f"session{i}", align_bytes=64) for i in range(NT)]
         for i in range(NT):
             nc.sync.dma_start(session[i][:], page1[i * P : (i + 1) * P, :])
         skip = keep.tile([P, PACK, S], F32, name="skip", tag="table0", align_bytes=64)
         for c in range(CHUNKS):
             for t in range(PACK):
-                bank = first_stage("skip_bank", c, e4m3_slice(w3_q, t))
+                bank = first_stage("b_bank", c, e4m3_slice(w3_q, t))
                 nc.scalar.copy(skip[:, t, c * CHUNK : (c + 1) * CHUNK], bank[:])
 
         spans = [(0, 256), (256, 512), (512, 1024)]
         prods = keep.tile([P, PACK, S], F32, name="prods", tag="table1", align_bytes=64)
 
+        late = []
+
         def weave(n):
             lo, hi = spans[n]
-            prod = prods[:, :, lo:hi]
+            prod = [prods[:, t, lo:hi] for t in range(PACK)]
             curved = prod
             if n == 1:
-                curved = keep.tile([P, PACK, hi - lo], F32, name="curved", tag="planes0", align_bytes=64)[:]
+                late.append(keep.tile([P, PACK, CHUNK], F32, name="late", tag="planes0", align_bytes=64))
+                curved = [late[0][:, t // 2, (t % 2) * 256 : (t % 2 + 1) * 256] for t in range(PACK)]
+            if n == 2:
+                prod = curved = prod[:2] + [late[0][:, t, :] for t in (2, 3)]
             planes = keep.tile([P, PACK, hi - lo], BF16, name="planes", tag=f"planes{n}", align_bytes=64)
             for t in range(PACK):
                 nc.vector.tensor_tensor(
-                    prod[:, t, :], pages[t][:].indirect(idx3[:, lo // 16 : hi // 16]), skip[:, t, lo:hi], ALU.mult
+                    prod[t], pages[t][:].indirect(idx3[:, lo // 16 : hi // 16]), skip[:, t, lo:hi], ALU.mult
                 )
-                nc.scalar.activation(curved[:, t, :], prod[:, t, :], ACT.Tanh)
-                nc.scalar.activation(planes[:, t, :], curved[:, t, :], ACT.Copy, scale=gain2_sb[:, t : t + 1])
+                nc.scalar.activation(curved[t], prod[t], ACT.Tanh)
+                nc.scalar.activation(planes[:, t, :], curved[t], ACT.Copy, scale=gain2_sb[:, t : t + 1])
             woven = ring.tile([P, hi - lo, PACK], BF16, name="woven", tag="rounded", align_bytes=64)
             nc.scalar.copy(
                 woven[:].rearrange("p (g i) t -> p g t i", i=4),
@@ -258,7 +267,7 @@ def tile_list_stutter_session_page_kernel(
 
         def put(n, i, z, y):
             lo, hi = spans[n]
-            y_bank = psum.tile([P, hi - lo], F32, name="y_bank", tag="y_bank")
+            y_bank = psum.tile([P, hi - lo], F32, name="y_bank", tag="b_bank", bufs=BANKS["b_bank"])
             nc.tensor.matmul_mx(
                 y_bank[:], lhsT=w4_codes[:, i * P : (i + 1) * P].bitcast(FP8X4),
                 lhsT_scale=w4_sc[:, i * P : (i + 1) * P],
@@ -275,7 +284,7 @@ def tile_list_stutter_session_page_kernel(
         for n, (lo, hi) in enumerate(spans):
             last = n == len(spans) - 1
             for i in range(NT if last else NT - 1):
-                put(n, i, z, ring.tile([P, hi - lo], F32, name="y", tag="y", bufs=NT))
+                put(n, i, z, ring.tile([P, hi - lo], F32, name="y", tag="y", bufs=NT - 1))
             if not last:
                 z_next = weave(n + 1)
                 put(n, NT - 1, z, keep.tile([P, hi - lo], F32, name="y_held", tag=f"planes{n + 1}", align_bytes=64))

@@ -1,6 +1,7 @@
 from contextlib import ExitStack
 
 import concourse.mybir as mybir
+from concourse.masks import make_identity
 
 K, T, S, H, T2, N = 1024, 4096, 1024, 512, 2048, 768
 FLOPS = 2 * (3 * K * H * S + H * N * S)
@@ -25,6 +26,7 @@ CHUNKS = S // CHUNK
 COLS = CHUNK // 16
 NT = N // P
 SCALE_BASE = 96
+UNIT = 256
 BANKS = {"a_bank": 2, "b_bank": 6}
 
 
@@ -59,13 +61,22 @@ def tile_list_stutter_session_page_kernel(
         nc.sync.dma_start(
             tab_sc[SCALE_BASE:P, :].bitcast(I32), tab_scales.rearrange("a q t -> (a q) t").bitcast(I32)
         )
-        w2_sc_raw = held([P, PASSES, H], U8, "w2_sc_raw")
-        nc.gpsimd.memset(w2_sc_raw[:].rearrange("p a c -> p (a c)").bitcast(I32), 0)
+        gain_rows = held([P, P], F32, "gain_rows")
+        nc.gpsimd.memset(gain_rows[:], 0.0)
+        w2_sc = held([P, PASSES, H], U8, "w2_sc")
+        nc.gpsimd.memset(w2_sc[:].rearrange("p a c -> p (a c)").bitcast(I32), 0)
         v_sc = [held([P, S], U8, f"v_sc{a}") for a in range(PASSES)]
         for a in range(PASSES):
             nc.gpsimd.memset(v_sc[a][:].bitcast(I32), 0)
         w4_sc = held([P, N], U8, "w4_sc")
         nc.gpsimd.memset(w4_sc[:].bitcast(I32), 0)
+
+        late_rows = held([P, P], F32, "late_rows")
+        nc.gpsimd.memset(late_rows[:], 0.0)
+        eye_bf16 = held([P, P], BF16, "eye_bf16")
+        make_identity(nc, eye_bf16[:])
+        eye_f32 = held([P, P], F32, "eye_f32")
+        make_identity(nc, eye_f32[:])
 
         picked_sc = held([P, S], U8, "picked_sc")
         nc.vector.tensor_copy(picked_sc[:], tab_sc[:].indirect(idx[:]))
@@ -84,17 +95,29 @@ def tile_list_stutter_session_page_kernel(
 
         def quantize_weight(raw, rounded, codes, name):
             nc.scalar.copy(
-                rounded.rearrange("p (t m j) -> p m t j", t=PACK, j=PACK),
-                raw[:].rearrange("p j (m t) -> p m t j", t=PACK),
+                rounded.rearrange("p (g i j) -> p g j i", i=4, j=PACK),
+                raw[:].rearrange("p j (g i) -> p g j i", i=4),
             )
             scales = held([P, H], U8, name + "_sc")
             nc.vector.quantize_mx(codes.bitcast(FP8X4), scales[:], rounded)
             return codes, scales
 
+        def load_columns(rows, vectors, name):
+            count = 0
+            for vec in vectors:
+                tiles = vec.shape[0] // P
+                nc.sync.dma_start(rows[count : count + tiles, :], vec.rearrange("(i p) -> i p", p=P))
+                count = count + tiles
+            bank = psum.tile([P, P], F32, name="bank", tag="b_bank", bufs=BANKS["b_bank"])
+            nc.tensor.transpose(bank[:], rows[:], eye_f32[:])
+            columns = held([P, count], F32, name)
+            nc.scalar.copy(columns[:], bank[:, 0:count])
+            return columns
+
         def load_w2_scales(quads):
             for q in quads:
                 nc.sync.dma_start(
-                    w2_sc_raw[32 * q : 32 * q + 4].bitcast(I32),
+                    w2_sc[32 * q : 32 * q + 4].bitcast(I32),
                     w2_scales[:, 4 * q : 4 * q + 4, :].rearrange("a r c -> r a c").bitcast(I32),
                 )
 
@@ -104,11 +127,8 @@ def tile_list_stutter_session_page_kernel(
             return table
 
         w1_raw = [load_weight(w1, a, f"session{2 + a}") for a in range(PASSES)]
-        w2_raw = held([P, PASSES, 2 * H], U8, "w2_raw")
-        nc.sync.dma_start(w2_raw[:].bitcast(I32), w2_words.rearrange("a p c -> p a c").bitcast(I32))
-        gain_sb = held([P, PACK], F32, "gain_sb")
-        nc.gpsimd.dma_start(gain_sb[:], gain.rearrange("(p t) -> p t", t=PACK))
         idx2 = load_list(offs2, "idx2")
+        gain_sb = load_columns(gain_rows, [gain], "gain_sb")
         load_w2_scales((0, 2, 1, 3))
         tables = [load_table(0)]
         place_scales(0, (0, 2, 1, 3))
@@ -121,18 +141,6 @@ def tile_list_stutter_session_page_kernel(
             rounded = ring.tile([P, PACK * H], BF16, name="rounded", tag="rounded", align_bytes=64)
             codes = held([P, H], U32, f"w1_codes{a}")
             w1_q.append(quantize_weight(w1_raw[a], rounded[:], codes[:], f"w1{a}"))
-
-        w2_codes = held([P, PASSES, 2 * H], U8, "w2_codes")
-        for a in range(PASSES):
-            nc.vector.tensor_copy(
-                w2_codes[:, a, :].rearrange("p (t m b) -> p t m b", t=PACK, b=2),
-                w2_raw[:, a, :].rearrange("p (m t b) -> p t m b", t=PACK, b=2),
-            )
-        w2_sc = held([P, PASSES, H], U8, "w2_sc")
-        nc.vector.tensor_copy(
-            w2_sc[:].rearrange("p a (t m) -> p a t m", t=PACK),
-            w2_sc_raw[:].rearrange("p a (m t) -> p a t m", t=PACK),
-        )
 
         v = {}
         for a in range(PASSES):
@@ -159,27 +167,17 @@ def tile_list_stutter_session_page_kernel(
                 w2_codes[:, a, 2 * t * P : 2 * (t + 1) * P].bitcast(FP4X4), w2_sc[:, a, t * P : (t + 1) * P]
             )
 
-        wgs_rows = wgs.rearrange("(q t) j -> q (t j)", t=PACK)
-        page0_rows = page0.rearrange("(p t) j -> p t j", t=PACK)
+        wgs_sb = held([P, S], F32, "wgs_sb")
+        nc.sync.dma_start(wgs_sb[:], wgs)
+        w2_codes = held([P, PASSES, 2 * H], U8, "w2_codes")
+        nc.sync.dma_start(w2_codes[:].bitcast(I32), w2_words.rearrange("a p c -> p a c").bitcast(I32))
         pages = [held([P, T2], F32, f"page{t}") for t in range(PACK)]
-        wg = {}
-
-        def load_wgs(first, last):
-            tile = held([P, (last - first) * CHUNK], F32, f"wgs{first}")
-            for q in (0, 2, 1, 3):
-                nc.sync.dma_start(tile[32 * q : 32 * (q + 1), :], wgs_rows[:, first * CHUNK : last * CHUNK])
-            for n in range(first, last):
-                wg[divmod(n, CHUNKS)] = tile[:, (n - first) * CHUNK : (n - first + 1) * CHUNK]
-
-        load_wgs(0, 1)
-        nc.sync.dma_start(pages[0][:], page0_rows[:, 0, :])
-        load_wgs(1, 4)
-        load_wgs(4, 8)
+        nc.sync.dma_start(pages[0][:], page0[0:P, :])
         w3_raw = [load_weight(w3, a, f"session{4 + a}") for a in range(PASSES)]
         for t in range(1, PACK):
-            nc.sync.dma_start(pages[t][:], page0_rows[:, t, :])
-        gain2_sb = held([P, PACK], F32, "gain2_sb")
-        nc.sync.dma_start(gain2_sb[:], gain2.rearrange("(p t) -> p t", t=PACK))
+            nc.sync.dma_start(pages[t][:], page0[t * P : (t + 1) * P, :])
+        late_columns = load_columns(late_rows, [gain2, bias], "late_columns")
+        gain2_sb, bias_sb = late_columns[:, 0:PACK], late_columns[:, PACK : PACK + NT]
         idx3 = load_list(offs3, "idx3")
         idx4 = load_list(offs4, "idx4")
         w4_codes = held([P, N], I32, "w4_codes")
@@ -190,15 +188,14 @@ def tile_list_stutter_session_page_kernel(
             )
         wgo_sb = held([P, S], F32, "wgo_sb")
         nc.sync.dma_start(wgo_sb[:], wgo)
-        bias_sb = held([P, NT], F32, "bias_sb")
-        with nc.allow_non_contiguous_dma(reason="one bias value for each partition and row tile"):
-            nc.sync.dma_start(bias_sb[:], bias.rearrange("(i p) -> p i", p=P))
 
         def new_states(t, c, least, scaled):
             a_bank = first_stage("a_bank", c, e4m3_slice(w1_q, t))
             b_bank = first_stage("b_bank", c, w2_slice(t))
             nc.scalar.activation(least, a_bank[:], ACT.Silu)
-            nc.scalar.activation(scaled, wg[t, c], ACT.Copy, scale=gain_sb[:, t : t + 1])
+            nc.scalar.activation(
+                scaled, wgs_sb[:, c * CHUNK : (c + 1) * CHUNK], ACT.Copy, scale=gain_sb[:, t : t + 1]
+            )
             nc.vector.tensor_tensor(least, b_bank[:], least, ALU.min)
 
         def renew(t, least_tag):
@@ -241,28 +238,48 @@ def tile_list_stutter_session_page_kernel(
 
         def weave(n):
             lo, hi = spans[n]
+            width = hi - lo
             prod = [prods[:, t, lo:hi] for t in range(PACK)]
             curved = prod
             if n == 1:
-                late.append(keep.tile([P, PACK, CHUNK], F32, name="late", tag="planes0", align_bytes=64))
-                curved = [late[0][:, t // 2, (t % 2) * 256 : (t % 2 + 1) * 256] for t in range(PACK)]
+                late.append(keep.tile([P, 6 * CHUNK], F32, name="late", tag="turned0", align_bytes=64))
+                curved = [late[0][:, t * width : (t + 1) * width] for t in range(PACK)]
             if n == 2:
-                prod = curved = prod[:2] + [late[0][:, t, :] for t in (2, 3)]
-            planes = keep.tile([P, PACK, hi - lo], BF16, name="planes", tag=f"planes{n}", align_bytes=64)
+                curved = [late[0][:, (2 + t) * width : (3 + t) * width] for t in range(PACK)]
+                prod = prod[:2] + curved[2:]
+            planes = ring.tile([P, PACK, width], BF16, name="planes", tag="planes", align_bytes=64)
             for t in range(PACK):
                 nc.vector.tensor_tensor(
                     prod[t], pages[t][:].indirect(idx3[:, lo // 16 : hi // 16]), skip[:, t, lo:hi], ALU.mult
                 )
                 nc.scalar.activation(curved[t], prod[t], ACT.Tanh)
                 nc.scalar.activation(planes[:, t, :], curved[t], ACT.Copy, scale=gain2_sb[:, t : t + 1])
-            woven = ring.tile([P, hi - lo, PACK], BF16, name="woven", tag="rounded", align_bytes=64)
-            nc.scalar.copy(
-                woven[:].rearrange("p (g i) t -> p g t i", i=4),
-                planes[:].rearrange("p t (g i) -> p g t i", i=4),
-            )
+            turned = keep.tile([P, PACK * width], BF16, name="turned", tag=f"turned{n}", align_bytes=64)
+            woven = ring.tile([P, PACK * width], BF16, name="woven", tag="rounded", align_bytes=64)
+            for unit in range(width // UNIT):
+                by_token = psum.tile([P, 2 * H], BF16, name="by_token", tag="a_bank", bufs=BANKS["a_bank"])
+                for b in range(2):
+                    for t in range(PACK):
+                        nc.tensor.transpose(
+                            by_token[:, b * H + t * P : b * H + (t + 1) * P],
+                            planes[:, t, unit * UNIT + b * P : unit * UNIT + (b + 1) * P],
+                            eye_bf16[:],
+                        )
+                nc.scalar.copy(turned[:, unit * 2 * H : (unit + 1) * 2 * H], by_token[:])
+                pairs = turned[:, unit * 2 * H : (unit + 1) * 2 * H].bitcast(F32)
+                by_row = psum.tile([P, 2, UNIT], F32, name="by_row", tag="b_bank", bufs=BANKS["b_bank"])
+                for b in range(2):
+                    for u in range(2):
+                        nc.tensor.transpose(
+                            by_row[:, u, b * P : (b + 1) * P], pairs[:, b * 2 * P + u : (b + 1) * 2 * P : 2], eye_f32[:]
+                        )
+                nc.scalar.copy(
+                    woven[:, unit * 2 * H : (unit + 1) * 2 * H].bitcast(F32).rearrange("p (j u) -> p j u", u=2),
+                    by_row[:].rearrange("p u j -> p j u"),
+                )
             z_codes = held([P, hi - lo], U32, f"z_codes{n}")
             z_sc = held([P, hi - lo], U8, f"z_sc{n}")
-            nc.vector.quantize_mx(z_codes[:].bitcast(FP8X4), z_sc[:], woven[:].rearrange("p j t -> p (j t)"))
+            nc.vector.quantize_mx(z_codes[:].bitcast(FP8X4), z_sc[:], woven[:])
             return z_codes, z_sc
 
         def put(n, i, z, y):
@@ -287,5 +304,5 @@ def tile_list_stutter_session_page_kernel(
                 put(n, i, z, ring.tile([P, hi - lo], F32, name="y", tag="y", bufs=NT - 1))
             if not last:
                 z_next = weave(n + 1)
-                put(n, NT - 1, z, keep.tile([P, hi - lo], F32, name="y_held", tag=f"planes{n + 1}", align_bytes=64))
+                put(n, NT - 1, z, keep.tile([P, hi - lo], F32, name="y_held", tag=f"turned{n + 1}", align_bytes=64))
                 z = z_next

@@ -19,15 +19,18 @@ ALU = mybir.AluOpType
 
 P = 128
 PACK = 4
-PASSES = K // (P * PACK)
-QUADS = 4
+K_PASS = P * PACK
+PASSES = K // K_PASS
+H_TILES = H // P
+N_TILES = N // P
+PER_COLUMN = 16
 CHUNK = 512
 CHUNKS = S // CHUNK
-COLS = CHUNK // 16
-NT = N // P
-SCALE_BASE = 96
-UNIT = 256
-BANKS = {"a_bank": 2, "b_bank": 6}
+UNIT = 2 * P
+SCALE_BASE = P - K // 32
+QUADS = (0, 2, 1, 3)
+BANKS = {"quick": 2, "waiting": 6}
+SPANS = [(0, 256), (256, 512), (512, 1024)]
 
 
 def tile_list_stutter_session_page_kernel(
@@ -41,28 +44,32 @@ def tile_list_stutter_session_page_kernel(
         ring = ctx.enter_context(tc.tile_pool(name="ring", bufs=2))
         psum = ctx.enter_context(tc.psum_pool(name="psum", bufs=2))
 
-        def held(shape, dtype, name):
-            return keep.tile(shape, dtype, name=name, align_bytes=64)
+        def held(shape, dtype, name, tag=""):
+            return keep.tile(shape, dtype, name=name, tag=tag or name, align_bytes=64)
+
+        def bank_of(shape, dtype, tag):
+            return psum.tile(shape, dtype, name="bank", tag=tag, bufs=BANKS[tag])
 
         def load_list(src, name):
-            tile = lists.tile([P, S // 16], U16, name=name)
+            tile = lists.tile([P, S // PER_COLUMN], U16, name=name)
             nc.sync.dma_start(tile[:], src)
             return tile
 
-        def chunk_of(lst, c):
-            return lst[:, c * COLS : (c + 1) * COLS]
+        def entries(lst, lo, hi):
+            return lst[:, lo // PER_COLUMN : hi // PER_COLUMN]
 
-        warm = held([P, 2], F32, "warm")
-        nc.vector.memset(warm[:, 0:1], 0.0)
-        nc.scalar.activation(warm[:, 1:2], warm[:, 0:1], ACT.Silu)
+        def plane_rows(plane, quad):
+            return plane[32 * quad : 32 * quad + 4].bitcast(I32)
+
         idx = load_list(offs, "idx")
         tab_sc = held([P, T], U8, "tab_sc")
         nc.vector.memset(tab_sc[0:SCALE_BASE, :].bitcast(I32), 0)
         nc.sync.dma_start(
-            tab_sc[SCALE_BASE:P, :].bitcast(I32), tab_scales.rearrange("a q t -> (a q) t").bitcast(I32)
+            tab_sc[SCALE_BASE:P, :].bitcast(I32), tab_scales.rearrange("a g t -> (a g) t").bitcast(I32)
         )
-        gain_rows = held([P, P], F32, "gain_rows")
-        nc.gpsimd.memset(gain_rows[:], 0.0)
+
+        vector_rows = held([P, P], F32, "vector_rows")
+        nc.gpsimd.memset(vector_rows[:], 0.0)
         w2_sc = held([P, PASSES, H], U8, "w2_sc")
         nc.gpsimd.memset(w2_sc[:].rearrange("p a c -> p (a c)").bitcast(I32), 0)
         v_sc = [held([P, S], U8, f"v_sc{a}") for a in range(PASSES)]
@@ -70,9 +77,6 @@ def tile_list_stutter_session_page_kernel(
             nc.gpsimd.memset(v_sc[a][:].bitcast(I32), 0)
         w4_sc = held([P, N], U8, "w4_sc")
         nc.gpsimd.memset(w4_sc[:].bitcast(I32), 0)
-
-        late_rows = held([P, P], F32, "late_rows")
-        nc.gpsimd.memset(late_rows[:], 0.0)
         eye_bf16 = held([P, P], BF16, "eye_bf16")
         make_identity(nc, eye_bf16[:])
         eye_f32 = held([P, P], F32, "eye_f32")
@@ -81,16 +85,26 @@ def tile_list_stutter_session_page_kernel(
         picked_sc = held([P, S], U8, "picked_sc")
         nc.vector.tensor_copy(picked_sc[:], tab_sc[:].indirect(idx[:]))
 
-        def place_scales(a, quads):
-            for q in quads:
-                row = SCALE_BASE + 16 * a + 4 * q
+        def place_scales(a):
+            for quad in QUADS:
+                row = SCALE_BASE + 16 * a + 4 * quad
+                nc.sync.dma_start(plane_rows(v_sc[a], quad), picked_sc[row : row + 4, :].bitcast(I32))
+
+        def load_w2_scales(quads):
+            for quad in quads:
                 nc.sync.dma_start(
-                    v_sc[a][32 * q : 32 * q + 4, :].bitcast(I32), picked_sc[row : row + 4, :].bitcast(I32)
+                    plane_rows(w2_sc, quad),
+                    w2_scales[:, 4 * quad : 4 * quad + 4, :].rearrange("a g c -> g a c").bitcast(I32),
                 )
 
+        def load_table(a):
+            table = held([P, T], I32, "table", f"table{a}")
+            nc.sync.dma_start(table[:], tab_words[a].rearrange("p t i -> p (t i)").bitcast(I32))
+            return table
+
         def load_weight(w, a, tag):
-            raw = keep.tile([P, PACK, H], F32, name="raw", tag=tag, align_bytes=64)
-            nc.sync.dma_start(raw[:], w[a * 512 : (a + 1) * 512, :].rearrange("(p j) c -> p j c", j=PACK))
+            raw = held([P, PACK, H], F32, "raw", tag)
+            nc.sync.dma_start(raw[:], w[a * K_PASS : (a + 1) * K_PASS, :].rearrange("(p j) c -> p j c", j=PACK))
             return raw
 
         def quantize_weight(raw, rounded, codes, name):
@@ -98,211 +112,200 @@ def tile_list_stutter_session_page_kernel(
                 rounded.rearrange("p (g i j) -> p g j i", i=4, j=PACK),
                 raw[:].rearrange("p j (g i) -> p g j i", i=4),
             )
-            scales = held([P, H], U8, name + "_sc")
+            scales = held([P, H], U8, name)
             nc.vector.quantize_mx(codes.bitcast(FP8X4), scales[:], rounded)
             return codes, scales
 
-        def load_columns(rows, vectors, name):
-            count = 0
-            for vec in vectors:
-                tiles = vec.shape[0] // P
-                nc.sync.dma_start(rows[count : count + tiles, :], vec.rearrange("(i p) -> i p", p=P))
-                count = count + tiles
-            bank = psum.tile([P, P], F32, name="bank", tag="b_bank", bufs=BANKS["b_bank"])
-            nc.tensor.transpose(bank[:], rows[:], eye_f32[:])
-            columns = held([P, count], F32, name)
-            nc.scalar.copy(columns[:], bank[:, 0:count])
-            return columns
-
-        def load_w2_scales(quads):
-            for q in quads:
-                nc.sync.dma_start(
-                    w2_sc[32 * q : 32 * q + 4].bitcast(I32),
-                    w2_scales[:, 4 * q : 4 * q + 4, :].rearrange("a r c -> r a c").bitcast(I32),
-                )
-
-        def load_table(a):
-            table = keep.tile([P, T], I32, name="table", tag=f"table{a}", align_bytes=64)
-            nc.sync.dma_start(table[:], tab_words[a].rearrange("p t i -> p (t i)").bitcast(I32))
-            return table
-
         w1_raw = [load_weight(w1, a, f"session{2 + a}") for a in range(PASSES)]
-        idx2 = load_list(offs2, "idx2")
-        gain_sb = load_columns(gain_rows, [gain], "gain_sb")
-        load_w2_scales((0, 2, 1, 3))
+
+        count = 0
+        for vec in (gain, gain2, bias):
+            tiles = vec.shape[0] // P
+            nc.sync.dma_start(vector_rows[count : count + tiles, :], vec.rearrange("(i p) -> i p", p=P))
+            count = count + tiles
+        columns_bank = bank_of([P, P], F32, "waiting")
+        nc.tensor.transpose(columns_bank[:], vector_rows[:], eye_f32[:])
+        columns = held([P, count], F32, "columns")
+        nc.scalar.copy(columns[:], columns_bank[:, 0:count])
+        gain_sb, gain2_sb = columns[:, 0:H_TILES], columns[:, H_TILES : 2 * H_TILES]
+        bias_sb = columns[:, 2 * H_TILES : count]
+
+        load_w2_scales(QUADS[:3])
         tables = [load_table(0)]
-        place_scales(0, (0, 2, 1, 3))
-        place_scales(1, (0, 2))
+        place_scales(0)
+        load_w2_scales(QUADS[3:])
+        wgs_sb = held([P, S], F32, "wgs_sb")
+        nc.sync.dma_start(wgs_sb[:], wgs)
+        w2_codes = held([P, PASSES, 2 * H], U8, "w2_codes")
+        nc.sync.dma_start(w2_codes[:].bitcast(I32), w2_words.rearrange("a p c -> p a c").bitcast(I32))
         tables.append(load_table(1))
-        place_scales(1, (1, 3))
+        place_scales(1)
+        idx2 = load_list(offs2, "idx2")
 
         w1_q = []
         for a in range(PASSES):
-            rounded = ring.tile([P, PACK * H], BF16, name="rounded", tag="rounded", align_bytes=64)
-            codes = held([P, H], U32, f"w1_codes{a}")
-            w1_q.append(quantize_weight(w1_raw[a], rounded[:], codes[:], f"w1{a}"))
+            w1_rounded = ring.tile([P, PACK * H], BF16, name="w1_rounded", tag="rounded", align_bytes=64)
+            w1_codes = held([P, H], U32, f"w1_codes{a}")
+            w1_q.append(quantize_weight(w1_raw[a], w1_rounded[:], w1_codes[:], f"w1_sc{a}"))
 
         v = {}
         for a in range(PASSES):
             for c in range(CHUNKS):
                 v[a, c] = held([P, CHUNK], U32, f"v{a}{c}")
-                nc.vector.tensor_copy(v[a, c][:], tables[a][:].bitcast(U32).indirect(chunk_of(idx, c)))
+                nc.vector.tensor_copy(
+                    v[a, c][:], tables[a][:].bitcast(U32).indirect(entries(idx, c * CHUNK, (c + 1) * CHUNK))
+                )
 
-        def first_stage(tag, c, weights):
-            bank = psum.tile([P, CHUNK], F32, name="bank", tag=tag, bufs=BANKS[tag])
+        def product(tag, c, weights):
+            bank = bank_of([P, CHUNK], F32, tag)
             for a in range(PASSES):
-                lhs, lhs_sc = weights(a)
+                codes, scales = weights(a)
                 nc.tensor.matmul_mx(
-                    bank[:], lhsT=lhs, lhsT_scale=lhs_sc,
+                    bank[:], lhsT=codes, lhsT_scale=scales,
                     rhs=v[a, c][:].bitcast(FP8X4), rhs_scale=v_sc[a][:, c * CHUNK : (c + 1) * CHUNK],
                     start=(a == 0), stop=(a == PASSES - 1),
                 )
             return bank
 
-        def e4m3_slice(q, t):
-            return lambda a: (q[a][0][:, t * P : (t + 1) * P].bitcast(FP8X4), q[a][1][:, t * P : (t + 1) * P])
+        def e4m3_tile(w_q, i):
+            return lambda a: (w_q[a][0][:, i * P : (i + 1) * P].bitcast(FP8X4), w_q[a][1][:, i * P : (i + 1) * P])
 
-        def w2_slice(t):
+        def w2_tile(i):
             return lambda a: (
-                w2_codes[:, a, 2 * t * P : 2 * (t + 1) * P].bitcast(FP4X4), w2_sc[:, a, t * P : (t + 1) * P]
+                w2_codes[:, a, 2 * i * P : 2 * (i + 1) * P].bitcast(FP4X4), w2_sc[:, a, i * P : (i + 1) * P]
             )
 
-        wgs_sb = held([P, S], F32, "wgs_sb")
-        nc.sync.dma_start(wgs_sb[:], wgs)
-        w2_codes = held([P, PASSES, 2 * H], U8, "w2_codes")
-        nc.sync.dma_start(w2_codes[:].bitcast(I32), w2_words.rearrange("a p c -> p a c").bitcast(I32))
-        pages = [held([P, T2], F32, f"page{t}") for t in range(PACK)]
+        pages = [held([P, T2], F32, f"page{i}") for i in range(H_TILES)]
         nc.sync.dma_start(pages[0][:], page0[0:P, :])
         w3_raw = [load_weight(w3, a, f"session{4 + a}") for a in range(PASSES)]
-        for t in range(1, PACK):
-            nc.sync.dma_start(pages[t][:], page0[t * P : (t + 1) * P, :])
-        late_columns = load_columns(late_rows, [gain2, bias], "late_columns")
-        gain2_sb, bias_sb = late_columns[:, 0:PACK], late_columns[:, PACK : PACK + NT]
+        for i in range(1, H_TILES):
+            nc.sync.dma_start(pages[i][:], page0[i * P : (i + 1) * P, :])
         idx3 = load_list(offs3, "idx3")
         idx4 = load_list(offs4, "idx4")
         w4_codes = held([P, N], I32, "w4_codes")
         nc.sync.dma_start(w4_codes[:], w4_words[0].rearrange("p c i -> p (c i)").bitcast(I32))
-        for q in range(QUADS):
-            nc.sync.dma_start(
-                w4_sc[32 * q : 32 * q + 4, :].bitcast(I32), w4_scales[0, 4 * q : 4 * q + 4, :].bitcast(I32)
-            )
+        for quad in QUADS:
+            nc.sync.dma_start(plane_rows(w4_sc, quad), w4_scales[0, 4 * quad : 4 * quad + 4, :].bitcast(I32))
         wgo_sb = held([P, S], F32, "wgo_sb")
         nc.sync.dma_start(wgo_sb[:], wgo)
 
-        def new_states(t, c, least, scaled):
-            a_bank = first_stage("a_bank", c, e4m3_slice(w1_q, t))
-            b_bank = first_stage("b_bank", c, w2_slice(t))
+        def new_states(i, c, least, scaled):
+            a_bank = product("quick", c, e4m3_tile(w1_q, i))
+            b_bank = product("waiting", c, w2_tile(i))
             nc.scalar.activation(least, a_bank[:], ACT.Silu)
             nc.scalar.activation(
-                scaled, wgs_sb[:, c * CHUNK : (c + 1) * CHUNK], ACT.Copy, scale=gain_sb[:, t : t + 1]
+                scaled, wgs_sb[:, c * CHUNK : (c + 1) * CHUNK], ACT.Copy, scale=gain_sb[:, i : i + 1]
             )
             nc.vector.tensor_tensor(least, b_bank[:], least, ALU.min)
 
-        def renew(t, least_tag):
-            least = keep.tile([P, S], F32, name="least", tag=least_tag, align_bytes=64)
+        for c in range(CHUNKS):
+            least = held([P, CHUNK], F32, f"least0{c}")
+            scaled = held([P, CHUNK], F32, f"scaled0{c}")
+            new_states(0, c, least[:], scaled[:])
+            nc.vector.tensor_tensor(
+                pages[0][:].indirect(entries(idx2, c * CHUNK, (c + 1) * CHUNK)), least[:], scaled[:], ALU.mult
+            )
+        scaled_rest = held([P, H_TILES - 1, S], F32, "scaled_rest", "least00")
+        for i in range(1, H_TILES):
+            least = held([P, S], F32, f"least{i}", "table1" if i == H_TILES - 1 else "")
             for c in range(CHUNKS):
                 cols = slice(c * CHUNK, (c + 1) * CHUNK)
-                new_states(t, c, least[:, cols], scaled_rest[:, t - 1, cols])
-            nc.vector.tensor_tensor(pages[t][:].indirect(idx2[:]), least[:], scaled_rest[:, t - 1, :], ALU.mult)
+                new_states(i, c, least[:, cols], scaled_rest[:, i - 1, cols])
+            nc.vector.tensor_tensor(pages[i][:].indirect(idx2[:]), least[:], scaled_rest[:, i - 1, :], ALU.mult)
 
-        for c in range(CHUNKS):
-            least = keep.tile([P, CHUNK], F32, name="least", tag=f"least0{c}", align_bytes=64)
-            scaled = keep.tile([P, CHUNK], F32, name="scaled", tag=f"scaled0{c}", align_bytes=64)
-            new_states(0, c, least[:], scaled[:])
-            nc.vector.tensor_tensor(pages[0][:].indirect(chunk_of(idx2, c)), least[:], scaled[:], ALU.mult)
-        scaled_rest = keep.tile([P, PACK - 1, S], F32, name="scaled_rest", tag="least00", align_bytes=64)
-        renew(1, "least1")
-        renew(2, "least2")
-        renew(3, "table1")
-        w3_rounded = keep.tile([P, PASSES * PACK * H], BF16, name="w3_rounded", tag="scaled00", align_bytes=64)
-        w3_codes = keep.tile([P, PASSES * H], U32, name="w3_codes", tag="least1", align_bytes=64)
+        w3_rounded = held([P, PASSES * PACK * H], BF16, "w3_rounded", "scaled00")
+        w3_codes = held([P, PASSES * H], U32, "w3_codes", "least1")
         w3_q = [
             quantize_weight(
-                w3_raw[a], w3_rounded[:, a * PACK * H : (a + 1) * PACK * H], w3_codes[:, a * H : (a + 1) * H], f"w3{a}"
+                w3_raw[a], w3_rounded[:, a * PACK * H : (a + 1) * PACK * H], w3_codes[:, a * H : (a + 1) * H],
+                f"w3_sc{a}",
             )
             for a in range(PASSES)
         ]
-        session = [keep.tile([P, T2], F32, name="session", tag=f"session{i}", align_bytes=64) for i in range(NT)]
-        for i in range(NT):
+        session = [held([P, T2], F32, "session", f"session{i}") for i in range(N_TILES)]
+        for i in range(N_TILES):
             nc.sync.dma_start(session[i][:], page1[i * P : (i + 1) * P, :])
-        skip = keep.tile([P, PACK, S], F32, name="skip", tag="table0", align_bytes=64)
+        skip = held([P, H_TILES, S], F32, "skip", "table0")
         for c in range(CHUNKS):
-            for t in range(PACK):
-                bank = first_stage("b_bank", c, e4m3_slice(w3_q, t))
-                nc.scalar.copy(skip[:, t, c * CHUNK : (c + 1) * CHUNK], bank[:])
+            for i in range(H_TILES):
+                skip_bank = product("waiting", c, e4m3_tile(w3_q, i))
+                nc.scalar.copy(skip[:, i, c * CHUNK : (c + 1) * CHUNK], skip_bank[:])
 
-        spans = [(0, 256), (256, 512), (512, 1024)]
-        prods = keep.tile([P, PACK, S], F32, name="prods", tag="table1", align_bytes=64)
+        prods = held([P, H_TILES, S], F32, "prods", "table1")
 
-        late = []
-
-        def weave(n):
-            lo, hi = spans[n]
+        def make_z(n, prod, curved):
+            lo, hi = SPANS[n]
             width = hi - lo
-            prod = [prods[:, t, lo:hi] for t in range(PACK)]
-            curved = prod
-            if n == 1:
-                late.append(keep.tile([P, 6 * CHUNK], F32, name="late", tag="turned0", align_bytes=64))
-                curved = [late[0][:, t * width : (t + 1) * width] for t in range(PACK)]
-            if n == 2:
-                curved = [late[0][:, (2 + t) * width : (3 + t) * width] for t in range(PACK)]
-                prod = prod[:2] + curved[2:]
-            planes = ring.tile([P, PACK, width], BF16, name="planes", tag="planes", align_bytes=64)
-            for t in range(PACK):
+            z_rows = ring.tile([P, H_TILES, width], BF16, name="z_rows", tag="z_rows", align_bytes=64)
+            for i in range(H_TILES):
                 nc.vector.tensor_tensor(
-                    prod[t], pages[t][:].indirect(idx3[:, lo // 16 : hi // 16]), skip[:, t, lo:hi], ALU.mult
+                    prod[i], pages[i][:].indirect(entries(idx3, lo, hi)), skip[:, i, lo:hi], ALU.mult
                 )
-                nc.scalar.activation(curved[t], prod[t], ACT.Tanh)
-                nc.scalar.activation(planes[:, t, :], curved[t], ACT.Copy, scale=gain2_sb[:, t : t + 1])
-            turned = keep.tile([P, PACK * width], BF16, name="turned", tag=f"turned{n}", align_bytes=64)
+                nc.scalar.activation(curved[i], prod[i], ACT.Tanh)
+                nc.scalar.activation(z_rows[:, i, :], curved[i], ACT.Copy, scale=gain2_sb[:, i : i + 1])
+            turned = held([P, PACK * width], BF16, "turned", f"turned{n}")
             woven = ring.tile([P, PACK * width], BF16, name="woven", tag="rounded", align_bytes=64)
             for unit in range(width // UNIT):
-                by_token = psum.tile([P, 2 * H], BF16, name="by_token", tag="a_bank", bufs=BANKS["a_bank"])
+                part = slice(unit * 2 * H, (unit + 1) * 2 * H)
+                by_entry = bank_of([P, 2 * H], BF16, "quick")
                 for b in range(2):
-                    for t in range(PACK):
+                    for i in range(H_TILES):
                         nc.tensor.transpose(
-                            by_token[:, b * H + t * P : b * H + (t + 1) * P],
-                            planes[:, t, unit * UNIT + b * P : unit * UNIT + (b + 1) * P],
+                            by_entry[:, b * H + i * P : b * H + (i + 1) * P],
+                            z_rows[:, i, unit * UNIT + b * P : unit * UNIT + (b + 1) * P],
                             eye_bf16[:],
                         )
-                nc.scalar.copy(turned[:, unit * 2 * H : (unit + 1) * 2 * H], by_token[:])
-                pairs = turned[:, unit * 2 * H : (unit + 1) * 2 * H].bitcast(F32)
-                by_row = psum.tile([P, 2, UNIT], F32, name="by_row", tag="b_bank", bufs=BANKS["b_bank"])
+                nc.scalar.copy(turned[:, part], by_entry[:])
+                pairs = turned[:, part].bitcast(F32)
+                by_row = bank_of([P, 2, UNIT], F32, "waiting")
                 for b in range(2):
                     for u in range(2):
                         nc.tensor.transpose(
                             by_row[:, u, b * P : (b + 1) * P], pairs[:, b * 2 * P + u : (b + 1) * 2 * P : 2], eye_f32[:]
                         )
                 nc.scalar.copy(
-                    woven[:, unit * 2 * H : (unit + 1) * 2 * H].bitcast(F32).rearrange("p (j u) -> p j u", u=2),
+                    woven[:, part].bitcast(F32).rearrange("p (j u) -> p j u", u=2),
                     by_row[:].rearrange("p u j -> p j u"),
                 )
-            z_codes = held([P, hi - lo], U32, f"z_codes{n}")
-            z_sc = held([P, hi - lo], U8, f"z_sc{n}")
+            z_codes = held([P, width], U32, f"z_codes{n}")
+            z_sc = held([P, width], U8, f"z_sc{n}")
             nc.vector.quantize_mx(z_codes[:].bitcast(FP8X4), z_sc[:], woven[:])
             return z_codes, z_sc
 
         def put(n, i, z, y):
-            lo, hi = spans[n]
-            y_bank = psum.tile([P, hi - lo], F32, name="y_bank", tag="b_bank", bufs=BANKS["b_bank"])
+            lo, hi = SPANS[n]
+            y_bank = bank_of([P, hi - lo], F32, "waiting")
             nc.tensor.matmul_mx(
                 y_bank[:], lhsT=w4_codes[:, i * P : (i + 1) * P].bitcast(FP8X4),
                 lhsT_scale=w4_sc[:, i * P : (i + 1) * P],
                 rhs=z[0][:].bitcast(FP8X4), rhs_scale=z[1][:], start=True, stop=True,
             )
             nc.scalar.activation(y[:], y_bank[:], ACT.Identity, bias=bias_sb[:, i : i + 1])
-            nc.vector.tensor_tensor(
-                session[i][:].indirect(idx4[:, lo // 16 : hi // 16]), y[:], wgo_sb[:, lo:hi], ALU.mult
-            )
+            nc.vector.tensor_tensor(session[i][:].indirect(entries(idx4, lo, hi)), y[:], wgo_sb[:, lo:hi], ALU.mult)
             if hi == S:
                 nc.sync.dma_start(out[i * P : (i + 1) * P, :], session[i][:])
 
-        z = weave(0)
-        for n, (lo, hi) in enumerate(spans):
-            last = n == len(spans) - 1
-            for i in range(NT if last else NT - 1):
-                put(n, i, z, ring.tile([P, hi - lo], F32, name="y", tag="y", bufs=NT - 1))
-            if not last:
-                z_next = weave(n + 1)
-                put(n, NT - 1, z, keep.tile([P, hi - lo], F32, name="y_held", tag=f"turned{n + 1}", align_bytes=64))
-                z = z_next
+        def put_from_ring(n, z, tiles):
+            width = SPANS[n][1] - SPANS[n][0]
+            for i in tiles:
+                put(n, i, z, ring.tile([P, width], F32, name="y", tag="y", bufs=N_TILES - 1))
+
+        def put_last(n, z):
+            width = SPANS[n][1] - SPANS[n][0]
+            put(n, N_TILES - 1, z, held([P, width], F32, "y_last", f"turned{n + 1}"))
+
+        span_prods = [[prods[:, i, lo:hi] for i in range(H_TILES)] for lo, hi in SPANS]
+        z0 = make_z(0, span_prods[0], span_prods[0])
+        put_from_ring(0, z0, range(N_TILES - 1))
+
+        width1, width2 = [hi - lo for lo, hi in SPANS[1:]]
+        late = held([P, H_TILES * (width1 + width2)], F32, "late", "turned0")
+        curved1 = [late[:, i * width1 : (i + 1) * width1] for i in range(H_TILES)]
+        start2 = H_TILES * width1
+        curved2 = [late[:, start2 + i * width2 : start2 + (i + 1) * width2] for i in range(H_TILES)]
+        z1 = make_z(1, span_prods[1], curved1)
+        put_last(0, z0)
+        put_from_ring(1, z1, range(N_TILES - 1))
+        z2 = make_z(2, span_prods[2][:2] + curved2[2:], curved2)
+        put_last(1, z1)
+        put_from_ring(2, z2, range(N_TILES))

from contextlib import ExitStack

import concourse.mybir as mybir
from concourse.masks import make_identity

K, T, S, H, T2, N = 1024, 4096, 1024, 512, 2048, 768
FLOPS = 2 * (3 * K * H * S + H * N * S)

F32 = mybir.dt.float32
BF16 = mybir.dt.bfloat16
I32 = mybir.dt.int32
U32 = mybir.dt.uint32
U16 = mybir.dt.uint16
U8 = mybir.dt.uint8
FP8X4 = mybir.dt.float8_e4m3fn_x4
FP4X4 = mybir.dt.float4_e2m1fn_x4
ACT = mybir.ActivationFunctionType
ALU = mybir.AluOpType

P = 128
PACK = 4
K_PASS = P * PACK
PASSES = K // K_PASS
H_TILES = H // P
N_TILES = N // P
PER_COLUMN = 16
CHUNK = 512
CHUNKS = S // CHUNK
UNIT = 2 * P
SCALE_BASE = P - K // 32
QUADS = (0, 2, 1, 3)
BANKS = {"quick": 2, "waiting": 6}
SPANS = [(0, 256), (256, 512), (512, 1024)]


def tile_list_stutter_session_page_kernel(
    tc, tab_words, tab_scales, offs, w1, w2_words, w2_scales, gain, wgs, page0, offs2, offs3,
    w3, gain2, w4_words, w4_scales, bias, wgo, page1, offs4, out,
):
    nc = tc.nc
    with ExitStack() as ctx:
        lists = ctx.enter_context(tc.tile_pool(name="lists", bufs=1))
        keep = ctx.enter_context(tc.tile_pool(name="keep", bufs=1))
        ring = ctx.enter_context(tc.tile_pool(name="ring", bufs=2))
        psum = ctx.enter_context(tc.psum_pool(name="psum", bufs=2))

        def held(shape, dtype, name, tag=""):
            return keep.tile(shape, dtype, name=name, tag=tag or name, align_bytes=64)

        def bank_of(shape, dtype, tag):
            return psum.tile(shape, dtype, name="bank", tag=tag, bufs=BANKS[tag])

        def load_list(src, name):
            tile = lists.tile([P, S // PER_COLUMN], U16, name=name)
            nc.sync.dma_start(tile[:], src)
            return tile

        def entries(lst, lo, hi):
            return lst[:, lo // PER_COLUMN : hi // PER_COLUMN]

        def plane_rows(plane, quad):
            return plane[32 * quad : 32 * quad + 4].bitcast(I32)

        idx = load_list(offs, "idx")
        tab_sc = held([P, T], U8, "tab_sc")
        nc.vector.memset(tab_sc[0:SCALE_BASE, :].bitcast(I32), 0)
        nc.sync.dma_start(
            tab_sc[SCALE_BASE:P, :].bitcast(I32), tab_scales.rearrange("a g t -> (a g) t").bitcast(I32)
        )

        vector_rows = held([P, P], F32, "vector_rows")
        nc.gpsimd.memset(vector_rows[:], 0.0)
        w2_sc = held([P, PASSES, H], U8, "w2_sc")
        nc.gpsimd.memset(w2_sc[:].rearrange("p a c -> p (a c)").bitcast(I32), 0)
        v_sc = [held([P, S], U8, f"v_sc{a}") for a in range(PASSES)]
        for a in range(PASSES):
            nc.gpsimd.memset(v_sc[a][:].bitcast(I32), 0)
        w4_sc = held([P, N], U8, "w4_sc")
        nc.gpsimd.memset(w4_sc[:].bitcast(I32), 0)
        eye_bf16 = held([P, P], BF16, "eye_bf16")
        make_identity(nc, eye_bf16[:])
        eye_f32 = held([P, P], F32, "eye_f32")
        make_identity(nc, eye_f32[:])

        picked_sc = held([P, S], U8, "picked_sc")
        nc.vector.tensor_copy(picked_sc[:], tab_sc[:].indirect(idx[:]))

        def place_scales(a):
            for quad in QUADS:
                row = SCALE_BASE + 16 * a + 4 * quad
                nc.sync.dma_start(plane_rows(v_sc[a], quad), picked_sc[row : row + 4, :].bitcast(I32))

        def load_w2_scales(quads):
            for quad in quads:
                nc.sync.dma_start(
                    plane_rows(w2_sc, quad),
                    w2_scales[:, 4 * quad : 4 * quad + 4, :].rearrange("a g c -> g a c").bitcast(I32),
                )

        def load_table(a):
            table = held([P, T], I32, "table", f"table{a}")
            nc.sync.dma_start(table[:], tab_words[a].rearrange("p t i -> p (t i)").bitcast(I32))
            return table

        def load_weight(w, a, tag):
            raw = held([P, PACK, H], F32, "raw", tag)
            nc.sync.dma_start(raw[:], w[a * K_PASS : (a + 1) * K_PASS, :].rearrange("(p j) c -> p j c", j=PACK))
            return raw

        def quantize_weight(raw, rounded, codes, name):
            nc.scalar.copy(
                rounded.rearrange("p (g i j) -> p g j i", i=4, j=PACK),
                raw[:].rearrange("p j (g i) -> p g j i", i=4),
            )
            scales = held([P, H], U8, name)
            nc.vector.quantize_mx(codes.bitcast(FP8X4), scales[:], rounded)
            return codes, scales

        w1_raw = [load_weight(w1, a, f"session{2 + a}") for a in range(PASSES)]

        count = 0
        for vec in (gain, gain2, bias):
            tiles = vec.shape[0] // P
            nc.sync.dma_start(vector_rows[count : count + tiles, :], vec.rearrange("(i p) -> i p", p=P))
            count = count + tiles
        columns_bank = bank_of([P, P], F32, "waiting")
        nc.tensor.transpose(columns_bank[:], vector_rows[:], eye_f32[:])
        columns = held([P, count], F32, "columns")
        nc.scalar.copy(columns[:], columns_bank[:, 0:count])
        gain_sb, gain2_sb = columns[:, 0:H_TILES], columns[:, H_TILES : 2 * H_TILES]
        bias_sb = columns[:, 2 * H_TILES : count]

        load_w2_scales(QUADS[:3])
        tables = [load_table(0)]
        place_scales(0)
        load_w2_scales(QUADS[3:])
        wgs_sb = held([P, S], F32, "wgs_sb")
        nc.sync.dma_start(wgs_sb[:], wgs)
        w2_codes = held([P, PASSES, 2 * H], U8, "w2_codes")
        nc.sync.dma_start(w2_codes[:].bitcast(I32), w2_words.rearrange("a p c -> p a c").bitcast(I32))
        tables.append(load_table(1))
        place_scales(1)
        idx2 = load_list(offs2, "idx2")

        w1_q = []
        for a in range(PASSES):
            w1_rounded = ring.tile([P, PACK * H], BF16, name="w1_rounded", tag="rounded", align_bytes=64)
            w1_codes = held([P, H], U32, f"w1_codes{a}")
            w1_q.append(quantize_weight(w1_raw[a], w1_rounded[:], w1_codes[:], f"w1_sc{a}"))

        v = {}
        for a in range(PASSES):
            for c in range(CHUNKS):
                v[a, c] = held([P, CHUNK], U32, f"v{a}{c}")
                nc.vector.tensor_copy(
                    v[a, c][:], tables[a][:].bitcast(U32).indirect(entries(idx, c * CHUNK, (c + 1) * CHUNK))
                )

        def product(tag, c, weights):
            bank = bank_of([P, CHUNK], F32, tag)
            for a in range(PASSES):
                codes, scales = weights(a)
                nc.tensor.matmul_mx(
                    bank[:], lhsT=codes, lhsT_scale=scales,
                    rhs=v[a, c][:].bitcast(FP8X4), rhs_scale=v_sc[a][:, c * CHUNK : (c + 1) * CHUNK],
                    start=(a == 0), stop=(a == PASSES - 1),
                )
            return bank

        def e4m3_tile(w_q, i):
            return lambda a: (w_q[a][0][:, i * P : (i + 1) * P].bitcast(FP8X4), w_q[a][1][:, i * P : (i + 1) * P])

        def w2_tile(i):
            return lambda a: (
                w2_codes[:, a, 2 * i * P : 2 * (i + 1) * P].bitcast(FP4X4), w2_sc[:, a, i * P : (i + 1) * P]
            )

        pages = [held([P, T2], F32, f"page{i}") for i in range(H_TILES)]
        nc.sync.dma_start(pages[0][:], page0[0:P, :])
        w3_raw = [load_weight(w3, a, f"session{4 + a}") for a in range(PASSES)]
        for i in range(1, H_TILES):
            nc.sync.dma_start(pages[i][:], page0[i * P : (i + 1) * P, :])
        idx3 = load_list(offs3, "idx3")
        idx4 = load_list(offs4, "idx4")
        w4_codes = held([P, N], I32, "w4_codes")
        nc.sync.dma_start(w4_codes[:], w4_words[0].rearrange("p c i -> p (c i)").bitcast(I32))
        for quad in QUADS:
            nc.sync.dma_start(plane_rows(w4_sc, quad), w4_scales[0, 4 * quad : 4 * quad + 4, :].bitcast(I32))
        wgo_sb = held([P, S], F32, "wgo_sb")
        nc.sync.dma_start(wgo_sb[:], wgo)

        def new_states(i, c, least, scaled):
            a_bank = product("quick", c, e4m3_tile(w1_q, i))
            b_bank = product("waiting", c, w2_tile(i))
            nc.scalar.activation(least, a_bank[:], ACT.Silu)
            nc.scalar.activation(
                scaled, wgs_sb[:, c * CHUNK : (c + 1) * CHUNK], ACT.Copy, scale=gain_sb[:, i : i + 1]
            )
            nc.vector.tensor_tensor(least, b_bank[:], least, ALU.min)

        for c in range(CHUNKS):
            least = held([P, CHUNK], F32, f"least0{c}")
            scaled = held([P, CHUNK], F32, f"scaled0{c}")
            new_states(0, c, least[:], scaled[:])
            nc.vector.tensor_tensor(
                pages[0][:].indirect(entries(idx2, c * CHUNK, (c + 1) * CHUNK)), least[:], scaled[:], ALU.mult
            )
        scaled_rest = held([P, H_TILES - 1, S], F32, "scaled_rest", "least00")
        for i in range(1, H_TILES):
            least = held([P, S], F32, f"least{i}", "table1" if i == H_TILES - 1 else "")
            for c in range(CHUNKS):
                cols = slice(c * CHUNK, (c + 1) * CHUNK)
                new_states(i, c, least[:, cols], scaled_rest[:, i - 1, cols])
            nc.vector.tensor_tensor(pages[i][:].indirect(idx2[:]), least[:], scaled_rest[:, i - 1, :], ALU.mult)

        w3_rounded = held([P, PASSES * PACK * H], BF16, "w3_rounded", "scaled00")
        w3_codes = held([P, PASSES * H], U32, "w3_codes", "least1")
        w3_q = [
            quantize_weight(
                w3_raw[a], w3_rounded[:, a * PACK * H : (a + 1) * PACK * H], w3_codes[:, a * H : (a + 1) * H],
                f"w3_sc{a}",
            )
            for a in range(PASSES)
        ]
        session = [held([P, T2], F32, "session", f"session{i}") for i in range(N_TILES)]
        for i in range(N_TILES):
            nc.sync.dma_start(session[i][:], page1[i * P : (i + 1) * P, :])
        skip = held([P, H_TILES, S], F32, "skip", "table0")
        for c in range(CHUNKS):
            for i in range(H_TILES):
                skip_bank = product("waiting", c, e4m3_tile(w3_q, i))
                nc.scalar.copy(skip[:, i, c * CHUNK : (c + 1) * CHUNK], skip_bank[:])

        prods = held([P, H_TILES, S], F32, "prods", "table1")

        def make_z(n, prod, curved):
            lo, hi = SPANS[n]
            width = hi - lo
            z_rows = ring.tile([P, H_TILES, width], BF16, name="z_rows", tag="z_rows", align_bytes=64)
            for i in range(H_TILES):
                nc.vector.tensor_tensor(
                    prod[i], pages[i][:].indirect(entries(idx3, lo, hi)), skip[:, i, lo:hi], ALU.mult
                )
                nc.scalar.activation(curved[i], prod[i], ACT.Tanh)
                nc.scalar.activation(z_rows[:, i, :], curved[i], ACT.Copy, scale=gain2_sb[:, i : i + 1])
            turned = held([P, PACK * width], BF16, "turned", f"turned{n}")
            woven = ring.tile([P, PACK * width], BF16, name="woven", tag="rounded", align_bytes=64)
            for unit in range(width // UNIT):
                part = slice(unit * 2 * H, (unit + 1) * 2 * H)
                by_entry = bank_of([P, 2 * H], BF16, "quick")
                for b in range(2):
                    for i in range(H_TILES):
                        nc.tensor.transpose(
                            by_entry[:, b * H + i * P : b * H + (i + 1) * P],
                            z_rows[:, i, unit * UNIT + b * P : unit * UNIT + (b + 1) * P],
                            eye_bf16[:],
                        )
                nc.scalar.copy(turned[:, part], by_entry[:])
                pairs = turned[:, part].bitcast(F32)
                by_row = bank_of([P, 2, UNIT], F32, "waiting")
                for b in range(2):
                    for u in range(2):
                        nc.tensor.transpose(
                            by_row[:, u, b * P : (b + 1) * P], pairs[:, b * 2 * P + u : (b + 1) * 2 * P : 2], eye_f32[:]
                        )
                nc.scalar.copy(
                    woven[:, part].bitcast(F32).rearrange("p (j u) -> p j u", u=2),
                    by_row[:].rearrange("p u j -> p j u"),
                )
            z_codes = held([P, width], U32, f"z_codes{n}")
            z_sc = held([P, width], U8, f"z_sc{n}")
            nc.vector.quantize_mx(z_codes[:].bitcast(FP8X4), z_sc[:], woven[:])
            return z_codes, z_sc

        def put(n, i, z, y):
            lo, hi = SPANS[n]
            y_bank = bank_of([P, hi - lo], F32, "waiting")
            nc.tensor.matmul_mx(
                y_bank[:], lhsT=w4_codes[:, i * P : (i + 1) * P].bitcast(FP8X4),
                lhsT_scale=w4_sc[:, i * P : (i + 1) * P],
                rhs=z[0][:].bitcast(FP8X4), rhs_scale=z[1][:], start=True, stop=True,
            )
            nc.scalar.activation(y[:], y_bank[:], ACT.Identity, bias=bias_sb[:, i : i + 1])
            nc.vector.tensor_tensor(session[i][:].indirect(entries(idx4, lo, hi)), y[:], wgo_sb[:, lo:hi], ALU.mult)
            if hi == S:
                nc.sync.dma_start(out[i * P : (i + 1) * P, :], session[i][:])

        def put_from_ring(n, z, tiles):
            width = SPANS[n][1] - SPANS[n][0]
            for i in tiles:
                put(n, i, z, ring.tile([P, width], F32, name="y", tag="y", bufs=N_TILES - 1))

        def put_last(n, z):
            width = SPANS[n][1] - SPANS[n][0]
            put(n, N_TILES - 1, z, held([P, width], F32, "y_last", f"turned{n + 1}"))

        span_prods = [[prods[:, i, lo:hi] for i in range(H_TILES)] for lo, hi in SPANS]
        z0 = make_z(0, span_prods[0], span_prods[0])
        put_from_ring(0, z0, range(N_TILES - 1))

        width1, width2 = [hi - lo for lo, hi in SPANS[1:]]
        late = held([P, H_TILES * (width1 + width2)], F32, "late", "turned0")
        curved1 = [late[:, i * width1 : (i + 1) * width1] for i in range(H_TILES)]
        start2 = H_TILES * width1
        curved2 = [late[:, start2 + i * width2 : start2 + (i + 1) * width2] for i in range(H_TILES)]
        z1 = make_z(1, span_prods[1], curved1)
        put_last(0, z0)
        put_from_ring(1, z1, range(N_TILES - 1))
        z2 = make_z(2, span_prods[2][:2] + curved2[2:], curved2)
        put_last(1, z1)
        put_from_ring(2, z2, range(N_TILES))
